import numpy as np
import ml_dtypes


def mxq(x, axis, fmt="e4m3"):
    dtype, down = {"e4m3": (ml_dtypes.float8_e4m3fn, 7), "e5m2": (ml_dtypes.float8_e5m2, 14)}[fmt]
    v = np.moveaxis(np.asarray(x, np.float32).astype(ml_dtypes.bfloat16).astype(np.float64), axis, -1)
    blocks = v.reshape(v.shape[:-1] + (-1, 32))
    amax = np.abs(blocks).max(-1, keepdims=True)
    byte = np.maximum(np.where(amax > 0, np.frexp(amax)[1] - 1 + 127, 0) - down, 1)
    scale = np.exp2(byte - 127.0)
    codes = (blocks / scale).astype(np.float32).astype(dtype).astype(np.float64)
    return np.moveaxis((codes * scale).reshape(v.shape), -1, axis)


WIDE = False


def mx_kscale(k):
    if not WIDE:
        return np.ones(k)
    levels = np.array([30, -30])
    if k % 512:
        return np.exp2(np.random.permutation(np.resize(levels, k // 32))).repeat(32)
    a = np.empty((k // 512, 16))
    for p in range(k // 512):
        a[p, :8] = np.random.permutation(np.resize(levels, 8))
        for g in range(8):
            far = levels[np.abs(levels - a[p, g]) >= 10]
            a[p, g + 8] = far[np.random.randint(len(far))]
    return np.exp2(a.ravel()).repeat(32)


BF16 = ml_dtypes.bfloat16


def bf(x):
    return np.asarray(x, np.float32).astype(BF16)


def f64(x):
    return np.asarray(x).astype(np.float64)


M, N, K, L = 1024, 2048, 512, 1536


def setup_inputs():
    s = mx_kscale(K)
    t = mx_kscale(L)
    tail = np.exp(0.5 * np.random.standard_normal((M, L)) - 0.25)
    return {
        "img_last": bf(np.random.standard_normal((M, K)) * s),
        "img_res": bf(np.random.standard_normal((M, L)) * tail),
        "gain": bf((1 + 0.1 * np.random.standard_normal(L)) * t),
        "txt_last": bf(0.7 * np.random.standard_normal((N, K)) / np.sqrt(K) / s),
        "txt_res": bf(0.7 * np.random.standard_normal((N, L)) / np.sqrt(L) / t),
        "bias": bf(0.3 * np.random.standard_normal(N)),
    }


def reference(img_last, img_res, gain, txt_last, txt_res, bias):
    a = mxq(f64(img_last), 1, "e4m3")
    b = mxq(f64(txt_last), 1, "e4m3")
    c = mxq(f64(img_res) * f64(gain), 1, "e5m2")
    d = mxq(f64(txt_res), 1, "e4m3")
    z = (a @ b.T) + (c @ d.T) + f64(bias)
    e = np.exp(z)
    return z, e.mean(axis=1), e.mean(axis=0)

@@ -1,0 +1,416 @@
+from contextlib import ExitStack
+
+import concourse.mybir as mybir
+from concourse.masks import make_identity
+
+F32 = mybir.dt.float32
+BF16 = mybir.dt.bfloat16
+U32 = mybir.dt.uint32
+U8 = mybir.dt.uint8
+E4M3 = mybir.dt.float8_e4m3fn_x4
+E5M2 = mybir.dt.float8_e5m2_x4
+ADD = mybir.AluOpType.add
+MULT = mybir.AluOpType.mult
+EXP = mybir.ActivationFunctionType.Exp
+X_AXIS = mybir.AxisListType.X
+
+P = 128
+IMAGES, TEXTS, LAST, RES = 1024, 2048, 512, 1536
+PASSES = (LAST + RES) // 512
+IMG_TILES = IMAGES // P
+BLOCKS = TEXTS // 512
+FLOPS = 2 * IMAGES * TEXTS * (LAST + RES)
+
+TILES = [("x", 0), ("x", 1), ("i", 0), ("x", 2), ("x", 3)] + [("i", m) for m in range(1, 8)] + [("x", t) for t in range(4, 16)]
+HEAD = 6
+TRANS_AFTER = {0: [6], 1: [7, 8], 2: [9], 3: [10, 12], 4: [11, 13], 5: [14, 15], 10: [16], 11: [17], 12: [18, 19], 18: [20, 21], 15: [22], 20: [23]}
+PERM = {7: (0, 's'), 8: (0, 's'), 9: (1, 's'), 10: (1, 's'), 13: (2, 's'), 14: (4, 's'), 15: (3, 's'), 16: (7, 's'), 17: (8, 'v'), 18: (10, 'v'), 19: (11, 's'), 20: (14, 's'), 21: (16, 's'), 22: (12, 's'), 23: (18, 's')}
+LOADS = [4, 5, 8, 2, 4]
+HEAD_BANKS = {0: "sv", 1: "sv", 3: "sv", 4: "sv"}
+BANKS = {12: 'vs', 13: 'ss', 14: 'ss', 15: 'ss', 16: 'vv', 17: 'vs', 18: 'sv', 19: 'sv', 20: 'sv', 21: 'sv', 22: 'sv', 23: 'ss'}
+SPREAD = {1: 1, 2: 9, 3: 6}
+COLSUM = [8, 8, 8, 1]
+FINISH = 13
+SINGLE = (0, 1, 2, 3)
+
+
+def tile_two_layer_contrastive_similarity_s2_kernel(
+    tc, img_last, img_res, gain, txt_last, txt_res, bias, out_0, out_1, out_2
+):
+    nc = tc.nc
+    with ExitStack() as ctx:
+        keep = ctx.enter_context(tc.tile_pool(name="keep", bufs=1))
+        ring2 = ctx.enter_context(tc.tile_pool(name="ring2", bufs=2))
+        ring3 = ctx.enter_context(tc.tile_pool(name="ring3", bufs=3))
+        ring6 = ctx.enter_context(tc.tile_pool(name="ring6", bufs=6))
+        tp_pool = ctx.enter_context(tc.psum_pool(name="tp_pool", bufs=4))
+        acc_pool = ctx.enter_context(tc.psum_pool(name="acc_pool", bufs=3))
+        misc_pool = ctx.enter_context(tc.psum_pool(name="misc_pool", bufs=1))
+        ctx.enter_context(tc.manual_schedule())
+
+        xl = [keep.tile([P, 4 * LAST], BF16, name=f"xl{b}", align_bytes=64) for b in range(BLOCKS)]
+        xr = [keep.tile([P, RES], BF16, name=f"xr{t}", align_bytes=64) for t in range(16)]
+        il = keep.tile([P, IMG_TILES * LAST], BF16, name="il", align_bytes=64)
+        ir = [keep.tile([P, RES], BF16, name=f"ir{m}", align_bytes=64) for m in range(IMG_TILES)]
+        img_last_v = img_last.rearrange("(p m) k -> p m k", m=IMG_TILES)
+        img_res_v = img_res.rearrange("(p m) k -> p m k", m=IMG_TILES)
+        out_v = out_0.rearrange("(p m) j -> p m j", m=IMG_TILES)
+
+        def load_xl(b, i0, i1):
+            nc.sync.dma_start(
+                out=xl[b][:, i0 * LAST : i1 * LAST].rearrange("p (i k) -> p i k", k=LAST),
+                in_=txt_last[b * 512 + i0 * P : b * 512 + i1 * P, :].rearrange("(i p) k -> p i k", p=P),
+            )
+
+        def load_xr(t):
+            nc.sync.dma_start(out=xr[t][:], in_=txt_res[t * P : (t + 1) * P, :])
+
+        def load_il(m0, m1):
+            nc.sync.dma_start(
+                out=il[:, m0 * LAST : m1 * LAST].rearrange("p (m k) -> p m k", k=LAST),
+                in_=img_last_v[:, m0:m1, :],
+            )
+
+        def load_ir(m):
+            nc.sync.dma_start(out=ir[m][:], in_=img_res_v[:, m, :])
+
+        warm = keep.tile([P, 1], F32, name="warm")
+        nc.vector.memset(warm[:], 0.0)
+        warm_out = keep.tile([P, 1], F32, name="warm_out")
+        nc.scalar.activation(out=warm_out[:], in_=warm[:], func=EXP)
+        bias_row = keep.tile([P, TEXTS], BF16, name="bias_row")
+        nc.vector.memset(bias_row[:], 0.0)
+        ones = keep.tile([P, P], BF16, name="ones")
+        nc.vector.memset(ones[:], 1.0)
+        col_w = keep.tile([P, 1], F32, name="col_w")
+        nc.vector.memset(col_w[:], 1.0 / IMAGES)
+        col_sums = keep.tile([P, P], F32, name="col_sums")
+        nc.vector.memset(col_sums[:], 0.0)
+        ident = keep.tile([P, P], F32, name="ident")
+        make_identity(nc, ident[:])
+        factors = keep.tile([P, 32], BF16, name="factors", align_bytes=64)
+        nc.gpsimd.dma_start(
+            out=factors[:, 4:16].rearrange("p (g t) -> p g t", t=4),
+            in_=gain.rearrange("(g p t) -> p g t", p=P, t=4),
+        )
+        nc.gpsimd.dma_start(out=bias_row[0:1, :], in_=bias.rearrange("(o k) -> o k", o=1))
+
+        load_xl(0, 0, 2)
+        load_xr(0)
+        load_xr(1)
+        load_il(0, 2)
+        load_ir(0)
+        load_xl(0, 2, 4)
+        load_xr(2)
+        load_xr(3)
+
+        load_ir(1)
+        load_il(2, 4)
+        load_ir(2)
+        load_ir(3)
+        load_il(4, 8)
+        for m in range(4, 8):
+            load_ir(m)
+
+        bias_b = keep.tile([P, TEXTS], BF16, name="bias_b", align_bytes=64)
+
+        def spread_bias(b):
+            spread = misc_pool.tile([P, 512], F32, name="misc")
+            nc.tensor.matmul(spread[:], ones[:], bias_row[:, b * 512 : (b + 1) * 512], start=True, stop=True)
+            return spread
+
+        def take_bias(b, spread):
+            nc.scalar.copy(out=bias_b[:, b * 512 : (b + 1) * 512], in_=spread[:])
+
+        x_codes = [keep.tile([P, PASSES, 512], U32, name=f"xc{b}", align_bytes=64) for b in range(BLOCKS)]
+        x_scales = [keep.tile([P, PASSES, 512], U8, name=f"xs{b}", align_bytes=64) for b in range(BLOCKS)]
+        i_codes = [keep.tile([P, PASSES, P], U32, name=f"ic{m}", align_bytes=64) for m in range(IMG_TILES)]
+        i_scales = [keep.tile([P, PASSES, P], U8, name=f"is{m}", align_bytes=64) for m in range(IMG_TILES)]
+        ready = {}
+        banks = {}
+        grouped_of = {}
+
+        def prep(a):
+            kind, n = TILES[a]
+            copy = nc.scalar.copy if PERM[a][1] == "s" else nc.vector.tensor_copy
+            x_perm = ring3.tile([P, PASSES * 512], BF16, name="x_perm", align_bytes=64)
+            words = x_perm[:].bitcast(F32).rearrange("p (g u w) -> p g u w", g=PASSES, u=2)
+            if kind == "x":
+                b, i = divmod(n, 4)
+                copy(
+                    out=words[:, 0, :, :],
+                    in_=xl[b][:, i * LAST : (i + 1) * LAST].bitcast(F32).rearrange("p (w u) -> p u w", u=2),
+                )
+            res = xr[n] if kind == "x" else ir[n]
+            copy(
+                out=words[:, 1:, :, :],
+                in_=res[:].bitcast(F32).rearrange("p (g w u) -> p g u w", g=3, u=2),
+            )
+            ready[a] = x_perm
+
+        def words_of(a, g, u):
+            kind, n = TILES[a]
+            if a in PERM and (kind == "x" or g > 0):
+                w = ready[a][:].bitcast(F32)
+                k = (g * 2 + u) * P
+                return w[:, k : k + P]
+            if kind == "i":
+                if g == 0:
+                    w = il[:].bitcast(F32)
+                    return w[:, n * 256 + u : (n + 1) * 256 : 2]
+                w = ir[n][:].bitcast(F32)
+                return w[:, (g - 1) * 256 + u : g * 256 : 2]
+            b, i = divmod(n, 4)
+            if g == 0:
+                w = xl[b][:].bitcast(F32)
+                return w[:, i * 256 + u : (i + 1) * 256 : 2]
+            w = xr[n][:].bitcast(F32)
+            return w[:, (g - 1) * 256 + u : g * 256 : 2]
+
+        def trans(a):
+            banks[a] = []
+            for h in range(2):
+                tp = tp_pool.tile([P, 2, 2, P], F32, name="tp")
+                for u in range(2):
+                    for j in range(2):
+                        nc.tensor.transpose(tp[:, u, j, :], words_of(a, 2 * h + j, u), ident[:])
+                banks[a].append(tp)
+
+        def copies(a, only):
+            kind, n = TILES[a]
+            if kind == "x":
+                engines = BANKS[a] if a in BANKS else HEAD_BANKS[a]
+                key, c0 = (("x", n), 0) if n in SINGLE else (n // 2, (n % 2) * P)
+                if key not in grouped_of:
+                    if n in SINGLE:
+                        grouped_of[key] = ring3.tile([P, PASSES * 512], BF16, name="grouped1", align_bytes=64)
+                    else:
+                        grouped_of[key] = ring2.tile([P, PASSES * 1024], BF16, name="x_grouped", align_bytes=64)
+                words = grouped_of[key][:].bitcast(F32).rearrange("p (g r u) -> p g r u", g=PASSES, u=2)
+                rows = slice(c0, c0 + P)
+                for h in range(2):
+                    if engines[h] != only:
+                        continue
+                    copy = nc.scalar.copy if only == "s" else nc.vector.tensor_copy
+                    copy(
+                        out=words[:, 2 * h : 2 * h + 2, rows, :],
+                        in_=banks[a][h][:].rearrange("p u g r -> p g r u"),
+                    )
+            else:
+                if ("i", a) not in grouped_of:
+                    grouped_of[("i", a)] = ring3.tile([P, PASSES * 512], BF16, name="grouped1", align_bytes=64)
+                i_grouped = grouped_of[("i", a)]
+                if only == "s":
+                    nc.scalar.copy(
+                        out=i_grouped[:, 0:512].bitcast(F32).rearrange("p (r u) -> p r u", u=2),
+                        in_=banks[a][0][:, :, 0, :].rearrange("p u r -> p r u"),
+                    )
+                    return
+                out = i_grouped[:].rearrange("p (g r u e) -> p g r u e", g=PASSES, u=2, e=2)
+                for h, j in ((0, 1), (1, 0)):
+                    g0, g1 = 2 * h + j, 2 * h + 2
+                    f = factors[:, 4 * g0 : 4 * g1].rearrange("p (g o u e) -> p g o u e", o=1, u=2, e=2)
+                    nc.vector.tensor_tensor(
+                        out=out[:, g0:g1],
+                        in0=banks[a][h][:, :, j:2, :].bitcast(BF16).rearrange("p u g (r e) -> p g r u e", e=2),
+                        in1=f.to_broadcast([P, g1 - g0, P, 2, 2]),
+                        op=MULT,
+                    )
+
+        def quant(a):
+            kind, n = TILES[a]
+            if kind == "x":
+                if n % 2 == 0 and n not in SINGLE:
+                    return
+                b, i = divmod(n, 4)
+                if n in SINGLE:
+                    grouped, c0 = grouped_of[("x", n)], i * P
+                else:
+                    grouped, c0 = grouped_of[n // 2], (i - 1) * P
+                c1 = (i + 1) * P
+                width = (c1 - c0) * 4
+                for g in range(PASSES):
+                    nc.vector.quantize_mx(
+                        out=x_codes[b][:, g, c0:c1].bitcast(E4M3),
+                        scales=x_scales[b][:, g, c0:c1],
+                        in_=grouped[:, g * width : (g + 1) * width],
+                    )
+            else:
+                grouped = grouped_of[("i", a)]
+                codes = i_codes[n][:].rearrange("p g r -> p (g r)")
+                scales = i_scales[n][:].rearrange("p g r -> p (g r)")
+                for g0, g1, fmt in ((0, 1, E4M3), (1, 3, E5M2), (3, 4, E5M2)):
+                    nc.vector.quantize_mx(
+                        out=codes[:, g0 * P : g1 * P].bitcast(fmt),
+                        scales=scales[:, g0 * P : g1 * P],
+                        in_=grouped[:, g0 * 512 : g1 * 512],
+                    )
+
+        acc_of = {}
+        z_of = {}
+        e_of = {}
+        sums = {}
+        row_sums = keep.tile([P, 7, BLOCKS], F32, name="row_sums")
+        last_sums = keep.tile([P, 5], F32, name="last_sums")
+        row_total = keep.tile([P, IMG_TILES], F32, name="row_total")
+        row_mean = keep.tile([P, IMG_TILES], F32, name="row_mean")
+
+        def mm(s):
+            b, m = divmod(s, IMG_TILES)
+            acc = acc_pool.tile([P, 512], F32, name="acc")
+            for g in range(PASSES):
+                nc.tensor.matmul_mx(
+                    out=acc[:],
+                    lhsT=i_codes[m][:, g, :].bitcast(E4M3 if g == 0 else E5M2),
+                    lhsT_scale=i_scales[m][:, g, :],
+                    rhs=x_codes[b][:, g, :].bitcast(E4M3),
+                    rhs_scale=x_scales[b][:, g, :],
+                    start=(g == 0),
+                    stop=(g == PASSES - 1),
+                )
+            acc_of[s] = acc
+
+        def zadd(s, c0=0, c1=512):
+            b, m = divmod(s, IMG_TILES)
+            if s not in z_of:
+                z_of[s] = ring6.tile([P, 512], F32, name="z")
+            nc.vector.tensor_tensor(
+                out=z_of[s][:, c0:c1], in0=acc_of[s][:, c0:c1], in1=bias_b[:, b * 512 + c0 : b * 512 + c1], op=ADD
+            )
+
+        def exp(s, c0=0, c1=512):
+            b, m = divmod(s, IMG_TILES)
+            if s not in e_of:
+                e_of[s] = ring6.tile([P, 512], F32, name="e")
+            part = last_sums[:, b + c0 // 256 : b + c0 // 256 + 1] if m == 7 else row_sums[:, m, b : b + 1]
+            nc.scalar.activation(out=e_of[s][:, c0:c1], in_=z_of[s][:, c0:c1], func=EXP, accum_out=part)
+
+        def store(s, c0=0, c1=512):
+            b, m = divmod(s, IMG_TILES)
+            nc.sync.dma_start(out=out_v[:, m, b * 512 + c0 : b * 512 + c1], in_=z_of[s][:, c0:c1])
+
+        def colsum(s):
+            b, m = divmod(s, IMG_TILES)
+            if m == 0 or s >= 30:
+                return
+            if m == 1:
+                first = e_of[s - 1]
+                total = ring2.tile([P, 512], F32, name="total")
+                sums[b] = total
+            else:
+                total = first = sums[b]
+            eng = nc.gpsimd if m < COLSUM[b] else nc.vector
+            eng.tensor_tensor(out=total[:], in0=first[:], in1=e_of[s][:], op=ADD)
+
+        def finish_cols(b, parts):
+            if b < BLOCKS:
+                cp = misc_pool.tile([P, 512], F32, name="misc")
+            else:
+                cp = acc_pool.tile([P, 512], F32, name="acc")
+            for c in range(4):
+                for n, part in enumerate(parts):
+                    nc.tensor.matmul(
+                        cp[:, c : c + 1],
+                        part[:, c * P : (c + 1) * P],
+                        col_w[:],
+                        start=(n == 0),
+                        stop=(n == len(parts) - 1),
+                    )
+            return cp
+
+        def take_cols(b, cp):
+            nc.vector.tensor_copy(out=col_sums[:, 4 * b : 4 * b + 4], in_=cp[:, 0:4])
+
+        for a in range(HEAD):
+            trans(a)
+            if a == 4:
+                spread = spread_bias(0)
+            copies(a, "s")
+            copies(a, "v")
+            quant(a)
+            if a == 4:
+                take_bias(0, spread)
+
+        pending = []
+        for b in range(1, BLOCKS):
+            pending.append(("xl", b))
+            for i in range(4):
+                pending.append(("xr", 4 * b + i))
+
+        def emit_loads(count):
+            for kind, n in pending[:count]:
+                if kind == "xl":
+                    load_xl(n, 0, 4)
+                else:
+                    load_xr(n)
+            pending[:count] = []
+
+        emit_loads(LOADS[0])
+        prev = []
+        old = []
+        late = []
+        spreads = []
+        for s in range(32):
+            mm(s)
+            for a in prev:
+                copies(a, "s")
+            for a in prev:
+                if TILES[a][0] == "i":
+                    copies(a, "v")
+            if s >= 1:
+                zadd(s - 1)
+                exp(s - 1)
+                store(s - 1)
+            for a in prev:
+                if TILES[a][0] == "i":
+                    quant(a)
+            for a in prev:
+                if TILES[a][0] == "x":
+                    copies(a, "v")
+            for a in old:
+                if TILES[a][0] == "x":
+                    quant(a)
+            for b, cp in late:
+                take_cols(b, cp)
+            late = []
+            for b, spread in spreads:
+                take_bias(b, spread)
+            spreads = []
+            emit_loads(LOADS[s + 1] if s + 1 < len(LOADS) else 3)
+            if s >= 2:
+                colsum(s - 2)
+            old = prev
+            prev = TRANS_AFTER.get(s, [])
+            for a in prev:
+                trans(a)
+            for a, at in PERM.items():
+                if at[0] == s:
+                    prep(a)
+            for b, at in SPREAD.items():
+                if at == s:
+                    spreads.append((b, spread_bias(b)))
+            if s >= FINISH and s % 8 == FINISH % 8:
+                late.append((s // 8 - 1, finish_cols(s // 8 - 1, [sums[s // 8 - 1]])))
+            if s == 31:
+                colsum(30)
+                col_part = keep.tile([P, 4], F32, name="col_part")
+                cp = finish_cols(3, [sums[3], e_of[30]])
+        zadd(31, 0, 256)
+        exp(31, 0, 256)
+        store(31, 0, 256)
+        zadd(31, 256, 512)
+        exp(31, 256, 512)
+        store(31, 256, 512)
+        nc.vector.tensor_copy(out=col_part[:], in_=cp[:, 0:4])
+        nc.vector.tensor_reduce(out=row_total[:, 0:7], in_=row_sums[:], axis=X_AXIS, op=ADD)
+        colsum(31)
+        last = finish_cols(4, [e_of[31]])
+        nc.vector.tensor_tensor(out=col_sums[:, 12:16], in0=last[:, 0:4], in1=col_part[:], op=ADD)
+        nc.vector.tensor_reduce(out=row_total[:, 7:8], in_=last_sums[:], axis=X_AXIS, op=ADD)
+        ct = acc_pool.tile([P, 512], F32, name="acc")
+        nc.tensor.transpose(ct[:, 0:P], col_sums[:], ident[:])
+        nc.vector.tensor_scalar(out=row_mean[:], in0=row_total[:], scalar1=1.0 / TEXTS, scalar2=None, op0=MULT)
+        nc.sync.dma_start(out=out_1.rearrange("(p m) -> p m", m=IMG_TILES), in_=row_mean[:])
+        col_mean = keep.tile([16, P], F32, name="col_mean")
+        nc.scalar.copy(out=col_mean[:], in_=ct[0:16, 0:P])
+        nc.sync.dma_start(out=out_2.rearrange("(c p) -> c p", p=P), in_=col_mean[:])

@@ -11,6 +11,7 @@ E4M3 = mybir.dt.float8_e4m3fn_x4
 E5M2 = mybir.dt.float8_e5m2_x4
 ADD = mybir.AluOpType.add
 MULT = mybir.AluOpType.mult
+COPY = mybir.ActivationFunctionType.Copy
 EXP = mybir.ActivationFunctionType.Exp
 X_AXIS = mybir.AxisListType.X
 
@@ -23,14 +24,16 @@ FLOPS = 2 * IMAGES * TEXTS * (LAST + RES)
 
 TILES = [("x", 0), ("x", 1), ("i", 0), ("x", 2), ("x", 3)] + [("i", m) for m in range(1, 8)] + [("x", t) for t in range(4, 16)]
 HEAD = 6
-TRANS_AFTER = {0: [6], 1: [7, 8], 2: [9], 3: [10, 12], 4: [11, 13], 5: [14, 15], 10: [16], 11: [17], 12: [18, 19], 18: [20, 21], 15: [22], 20: [23]}
-PERM = {7: (0, 's'), 8: (0, 's'), 9: (1, 's'), 10: (1, 's'), 13: (2, 's'), 14: (4, 's'), 15: (3, 's'), 16: (7, 's'), 17: (8, 'v'), 18: (10, 'v'), 19: (11, 's'), 20: (14, 's'), 21: (16, 's'), 22: (12, 's'), 23: (18, 's')}
-LOADS = [4, 5, 8, 2, 4]
+TRANS_AFTER = {0: [6], 1: [7, 8], 2: [9, 10], 4: [11, 14], 3: [12, 13], 5: [15], 7: [16], 12: [17, 18], 13: [19], 19: [20, 23], 20: [21], 15: [22]}
+PERM = {7: (0, 's'), 9: (1, 's'), 10: (1, 's'), 11: (3, 's'), 14: (3, 's'), 15: (4, 'v'), 16: (4, 's'), 17: (10, 'v'), 18: (10, 's'), 19: (11, 's'), 20: (16, 's'), 21: (19, 'v'), 23: (16, 's')}
+LOADS = [2, 2, 2, 3, 2]
 HEAD_BANKS = {0: "sv", 1: "sv", 3: "sv", 4: "sv"}
-BANKS = {12: 'vs', 13: 'ss', 14: 'ss', 15: 'ss', 16: 'vv', 17: 'vs', 18: 'sv', 19: 'sv', 20: 'sv', 21: 'sv', 22: 'sv', 23: 'ss'}
-SPREAD = {1: 1, 2: 9, 3: 6}
-COLSUM = [8, 8, 8, 1]
-FINISH = 13
+X_BUFS = 8
+Z_BUFS = 12
+BANKS = {6: 'ss', 7: 'vv', 8: 'sv', 9: 'vs', 10: 'sv', 11: 'vv', 12: 'vs', 13: 'vv', 14: 'ss', 15: 'ss', 16: 'ss', 17: 'vs', 18: 'ss', 19: 'ss', 20: 'vv', 21: 'ss', 22: 'ss', 23: 'ss'}
+SPREAD = {1: 3, 2: 1, 3: 7}
+COLSUM = [8, 8, 8, 5]
+FINISH = 12
 SINGLE = (0, 1, 2, 3)
 
 
@@ -42,14 +45,16 @@ def tile_two_layer_contrastive_similarity_s2_kernel(
         keep = ctx.enter_context(tc.tile_pool(name="keep", bufs=1))
         ring2 = ctx.enter_context(tc.tile_pool(name="ring2", bufs=2))
         ring3 = ctx.enter_context(tc.tile_pool(name="ring3", bufs=3))
-        ring6 = ctx.enter_context(tc.tile_pool(name="ring6", bufs=6))
+        x_ring = ctx.enter_context(tc.tile_pool(name="x_ring", bufs=X_BUFS))
+        z_ring = ctx.enter_context(tc.tile_pool(name="z_ring", bufs=Z_BUFS))
+        e_ring = ctx.enter_context(tc.tile_pool(name="e_ring", bufs=6))
         tp_pool = ctx.enter_context(tc.psum_pool(name="tp_pool", bufs=4))
         acc_pool = ctx.enter_context(tc.psum_pool(name="acc_pool", bufs=3))
         misc_pool = ctx.enter_context(tc.psum_pool(name="misc_pool", bufs=1))
         ctx.enter_context(tc.manual_schedule())
 
         xl = [keep.tile([P, 4 * LAST], BF16, name=f"xl{b}", align_bytes=64) for b in range(BLOCKS)]
-        xr = [keep.tile([P, RES], BF16, name=f"xr{t}", align_bytes=64) for t in range(16)]
+        xr = {}
         il = keep.tile([P, IMG_TILES * LAST], BF16, name="il", align_bytes=64)
         ir = [keep.tile([P, RES], BF16, name=f"ir{m}", align_bytes=64) for m in range(IMG_TILES)]
         img_last_v = img_last.rearrange("(p m) k -> p m k", m=IMG_TILES)
@@ -63,6 +68,8 @@ def tile_two_layer_contrastive_similarity_s2_kernel(
             )
 
         def load_xr(t):
+            x_res = x_ring.tile([P, RES], BF16, name="x_res", align_bytes=64)
+            xr[t] = x_res
             nc.sync.dma_start(out=xr[t][:], in_=txt_res[t * P : (t + 1) * P, :])
 
         def load_il(m0, m1):
@@ -74,27 +81,24 @@ def tile_two_layer_contrastive_similarity_s2_kernel(
         def load_ir(m):
             nc.sync.dma_start(out=ir[m][:], in_=img_res_v[:, m, :])
 
+        ident = keep.tile([P, P], F32, name="ident")
+        make_identity(nc, ident[:])
         warm = keep.tile([P, 1], F32, name="warm")
         nc.vector.memset(warm[:], 0.0)
         warm_out = keep.tile([P, 1], F32, name="warm_out")
         nc.scalar.activation(out=warm_out[:], in_=warm[:], func=EXP)
-        bias_row = keep.tile([P, TEXTS], BF16, name="bias_row")
-        nc.vector.memset(bias_row[:], 0.0)
-        ones = keep.tile([P, P], BF16, name="ones")
-        nc.vector.memset(ones[:], 1.0)
-        col_w = keep.tile([P, 1], F32, name="col_w")
-        nc.vector.memset(col_w[:], 1.0 / IMAGES)
-        col_sums = keep.tile([P, P], F32, name="col_sums")
-        nc.vector.memset(col_sums[:], 0.0)
-        ident = keep.tile([P, P], F32, name="ident")
-        make_identity(nc, ident[:])
-        factors = keep.tile([P, 32], BF16, name="factors", align_bytes=64)
+        factors = keep.tile([P, 12], BF16, name="factors", align_bytes=64)
         nc.gpsimd.dma_start(
-            out=factors[:, 4:16].rearrange("p (g t) -> p g t", t=4),
+            out=factors[:].rearrange("p (g t) -> p g t", t=4),
             in_=gain.rearrange("(g p t) -> p g t", p=P, t=4),
         )
+        bias_row = keep.tile([P, TEXTS], BF16, name="bias_row")
+        nc.vector.memset(bias_row[:], 0.0)
         nc.gpsimd.dma_start(out=bias_row[0:1, :], in_=bias.rearrange("(o k) -> o k", o=1))
-
+        ones = keep.tile([P, P], BF16, name="ones")
+        nc.vector.memset(ones[:], 1.0)
+        col_sums = keep.tile([P, P], F32, name="col_sums")
+        nc.vector.memset(col_sums[:], 0.0)
         load_xl(0, 0, 2)
         load_xr(0)
         load_xr(1)
@@ -132,39 +136,36 @@ def tile_two_layer_contrastive_similarity_s2_kernel(
 
         def prep(a):
             kind, n = TILES[a]
-            copy = nc.scalar.copy if PERM[a][1] == "s" else nc.vector.tensor_copy
             x_perm = ring3.tile([P, PASSES * 512], BF16, name="x_perm", align_bytes=64)
-            words = x_perm[:].bitcast(F32).rearrange("p (g u w) -> p g u w", g=PASSES, u=2)
+            ready[a] = x_perm
+            copy = nc.scalar.copy if PERM[a][1] == "s" else nc.vector.tensor_copy
+            words = x_perm[:].bitcast(F32)
             if kind == "x":
                 b, i = divmod(n, 4)
                 copy(
-                    out=words[:, 0, :, :],
+                    out=words[:, 768:1024].rearrange("p (u w) -> p u w", u=2),
                     in_=xl[b][:, i * LAST : (i + 1) * LAST].bitcast(F32).rearrange("p (w u) -> p u w", u=2),
                 )
             res = xr[n] if kind == "x" else ir[n]
             copy(
-                out=words[:, 1:, :, :],
-                in_=res[:].bitcast(F32).rearrange("p (g w u) -> p g u w", g=3, u=2),
+                out=words[:, 0:768].rearrange("p (u w) -> p u w", u=2),
+                in_=res[:].bitcast(F32).rearrange("p (w u) -> p u w", u=2),
             )
-            ready[a] = x_perm
 
         def words_of(a, g, u):
             kind, n = TILES[a]
-            if a in PERM and (kind == "x" or g > 0):
+            if kind == "i" and g == 0:
+                w = il[:].bitcast(F32)
+                return w[:, n * 256 + u : (n + 1) * 256 : 2]
+            if a in ready:
                 w = ready[a][:].bitcast(F32)
-                k = (g * 2 + u) * P
+                k = 768 + u * P if g == 0 else u * 384 + (g - 1) * P
                 return w[:, k : k + P]
-            if kind == "i":
-                if g == 0:
-                    w = il[:].bitcast(F32)
-                    return w[:, n * 256 + u : (n + 1) * 256 : 2]
-                w = ir[n][:].bitcast(F32)
-                return w[:, (g - 1) * 256 + u : g * 256 : 2]
             b, i = divmod(n, 4)
             if g == 0:
                 w = xl[b][:].bitcast(F32)
                 return w[:, i * 256 + u : (i + 1) * 256 : 2]
-            w = xr[n][:].bitcast(F32)
+            w = (xr[n] if kind == "x" else ir[n])[:].bitcast(F32)
             return w[:, (g - 1) * 256 + u : g * 256 : 2]
 
         def trans(a):
@@ -178,43 +179,36 @@ def tile_two_layer_contrastive_similarity_s2_kernel(
 
         def copies(a, only):
             kind, n = TILES[a]
-            if kind == "x":
-                engines = BANKS[a] if a in BANKS else HEAD_BANKS[a]
-                key, c0 = (("x", n), 0) if n in SINGLE else (n // 2, (n % 2) * P)
-                if key not in grouped_of:
-                    if n in SINGLE:
-                        grouped_of[key] = ring3.tile([P, PASSES * 512], BF16, name="grouped1", align_bytes=64)
-                    else:
-                        grouped_of[key] = ring2.tile([P, PASSES * 1024], BF16, name="x_grouped", align_bytes=64)
-                words = grouped_of[key][:].bitcast(F32).rearrange("p (g r u) -> p g r u", g=PASSES, u=2)
-                rows = slice(c0, c0 + P)
-                for h in range(2):
-                    if engines[h] != only:
-                        continue
-                    copy = nc.scalar.copy if only == "s" else nc.vector.tensor_copy
-                    copy(
-                        out=words[:, 2 * h : 2 * h + 2, rows, :],
-                        in_=banks[a][h][:].rearrange("p u g r -> p g r u"),
-                    )
-            else:
-                if ("i", a) not in grouped_of:
-                    grouped_of[("i", a)] = ring3.tile([P, PASSES * 512], BF16, name="grouped1", align_bytes=64)
-                i_grouped = grouped_of[("i", a)]
+            engines = BANKS[a] if a in BANKS else HEAD_BANKS.get(a, "")
+            single = kind == "i" or n in SINGLE
+            key, r0 = (a, 0) if single else (("pair", n // 2), (n % 2) * P)
+            if key not in grouped_of:
+                if single:
+                    grouped_of[key] = ring3.tile([P, PASSES * 512], BF16, name="grouped1", align_bytes=64)
+                else:
+                    grouped_of[key] = ring2.tile([P, PASSES * 1024], BF16, name="grouped2", align_bytes=64)
+            words = grouped_of[key][:].bitcast(F32).rearrange("p (g r u) -> p g r u", g=PASSES, u=2)
+            if kind == "i":
                 if only == "s":
-                    nc.scalar.copy(
-                        out=i_grouped[:, 0:512].bitcast(F32).rearrange("p (r u) -> p r u", u=2),
-                        in_=banks[a][0][:, :, 0, :].rearrange("p u r -> p r u"),
-                    )
+                    nc.scalar.copy(out=words[:, 0], in_=banks[a][0][:, :, 0, :].rearrange("p u r -> p r u"))
                     return
-                out = i_grouped[:].rearrange("p (g r u e) -> p g r u e", g=PASSES, u=2, e=2)
+                out = grouped_of[key][:].rearrange("p (g r u e) -> p g r u e", g=PASSES, u=2, e=2)
                 for h, j in ((0, 1), (1, 0)):
                     g0, g1 = 2 * h + j, 2 * h + 2
-                    f = factors[:, 4 * g0 : 4 * g1].rearrange("p (g o u e) -> p g o u e", o=1, u=2, e=2)
+                    f = factors[:, 4 * g0 - 4 : 4 * g1 - 4].rearrange("p (g o u e) -> p g o u e", o=1, u=2, e=2)
                     nc.vector.tensor_tensor(
                         out=out[:, g0:g1],
                         in0=banks[a][h][:, :, j:2, :].bitcast(BF16).rearrange("p u g (r e) -> p g r u e", e=2),
                         in1=f.to_broadcast([P, g1 - g0, P, 2, 2]),
                         op=MULT,
+                    )
+                return
+            for h in range(2):
+                if engines[h] == only:
+                    copy = nc.scalar.copy if only == "s" else nc.vector.tensor_copy
+                    copy(
+                        out=words[:, 2 * h : 2 * h + 2, r0 : r0 + P, :],
+                        in_=banks[a][h][:].rearrange("p u g r -> p g r u"),
                     )
 
         def quant(a):
@@ -224,9 +218,9 @@ def tile_two_layer_contrastive_similarity_s2_kernel(
                     return
                 b, i = divmod(n, 4)
                 if n in SINGLE:
-                    grouped, c0 = grouped_of[("x", n)], i * P
+                    grouped, c0 = grouped_of[a], i * P
                 else:
-                    grouped, c0 = grouped_of[n // 2], (i - 1) * P
+                    grouped, c0 = grouped_of["pair", n // 2], (i - 1) * P
                 c1 = (i + 1) * P
                 width = (c1 - c0) * 4
                 for g in range(PASSES):
@@ -236,7 +230,7 @@ def tile_two_layer_contrastive_similarity_s2_kernel(
                         in_=grouped[:, g * width : (g + 1) * width],
                     )
             else:
-                grouped = grouped_of[("i", a)]
+                grouped = grouped_of[a]
                 codes = i_codes[n][:].rearrange("p g r -> p (g r)")
                 scales = i_scales[n][:].rearrange("p g r -> p (g r)")
                 for g0, g1, fmt in ((0, 1, E4M3), (1, 3, E5M2), (3, 4, E5M2)):
@@ -252,6 +246,7 @@ def tile_two_layer_contrastive_similarity_s2_kernel(
         sums = {}
         row_sums = keep.tile([P, 7, BLOCKS], F32, name="row_sums")
         last_sums = keep.tile([P, 5], F32, name="last_sums")
+        parts = keep.tile([P, 4, 3], F32, name="parts")
         row_total = keep.tile([P, IMG_TILES], F32, name="row_total")
         row_mean = keep.tile([P, IMG_TILES], F32, name="row_mean")
 
@@ -273,7 +268,7 @@ def tile_two_layer_contrastive_similarity_s2_kernel(
         def zadd(s, c0=0, c1=512):
             b, m = divmod(s, IMG_TILES)
             if s not in z_of:
-                z_of[s] = ring6.tile([P, 512], F32, name="z")
+                z_of[s] = z_ring.tile([P, 512], F32, name="z")
             nc.vector.tensor_tensor(
                 out=z_of[s][:, c0:c1], in0=acc_of[s][:, c0:c1], in1=bias_b[:, b * 512 + c0 : b * 512 + c1], op=ADD
             )
@@ -281,7 +276,7 @@ def tile_two_layer_contrastive_similarity_s2_kernel(
         def exp(s, c0=0, c1=512):
             b, m = divmod(s, IMG_TILES)
             if s not in e_of:
-                e_of[s] = ring6.tile([P, 512], F32, name="e")
+                e_of[s] = e_ring.tile([P, 512], F32, name="e")
             part = last_sums[:, b + c0 // 256 : b + c0 // 256 + 1] if m == 7 else row_sums[:, m, b : b + 1]
             nc.scalar.activation(out=e_of[s][:, c0:c1], in_=z_of[s][:, c0:c1], func=EXP, accum_out=part)
 
@@ -289,7 +284,7 @@ def tile_two_layer_contrastive_similarity_s2_kernel(
             b, m = divmod(s, IMG_TILES)
             nc.sync.dma_start(out=out_v[:, m, b * 512 + c0 : b * 512 + c1], in_=z_of[s][:, c0:c1])
 
-        def colsum(s):
+        def colsum(s, c0=0, c1=512):
             b, m = divmod(s, IMG_TILES)
             if m == 0 or s >= 30:
                 return
@@ -300,26 +295,14 @@ def tile_two_layer_contrastive_similarity_s2_kernel(
             else:
                 total = first = sums[b]
             eng = nc.gpsimd if m < COLSUM[b] else nc.vector
-            eng.tensor_tensor(out=total[:], in0=first[:], in1=e_of[s][:], op=ADD)
+            eng.tensor_tensor(out=total[:, c0:c1], in0=first[:, c0:c1], in1=e_of[s][:, c0:c1], op=ADD)
 
-        def finish_cols(b, parts):
-            if b < BLOCKS:
-                cp = misc_pool.tile([P, 512], F32, name="misc")
-            else:
-                cp = acc_pool.tile([P, 512], F32, name="acc")
-            for c in range(4):
-                for n, part in enumerate(parts):
-                    nc.tensor.matmul(
-                        cp[:, c : c + 1],
-                        part[:, c * P : (c + 1) * P],
-                        col_w[:],
-                        start=(n == 0),
-                        stop=(n == len(parts) - 1),
-                    )
-            return cp
+        def turn_cols(source, turned, c0=0, c1=4):
+            for c in range(c0, c1):
+                nc.tensor.transpose(turned[:, c, :], source[:, c * P : (c + 1) * P], ident[:])
 
-        def take_cols(b, cp):
-            nc.vector.tensor_copy(out=col_sums[:, 4 * b : 4 * b + 4], in_=cp[:, 0:4])
+        def take_cols(out, turned):
+            nc.vector.tensor_reduce(out=out, in_=turned, axis=X_AXIS, op=ADD)
 
         for a in range(HEAD):
             trans(a)
@@ -345,6 +328,11 @@ def tile_two_layer_contrastive_similarity_s2_kernel(
                     load_xr(n)
             pending[:count] = []
 
+        def preps(s):
+            for a in range(6, 24):
+                if a in PERM and PERM[a][0] == s:
+                    prep(a)
+
         emit_loads(LOADS[0])
         prev = []
         old = []
@@ -368,10 +356,9 @@ def tile_two_layer_contrastive_similarity_s2_kernel(
                 if TILES[a][0] == "x":
                     copies(a, "v")
             for a in old:
-                if TILES[a][0] == "x":
-                    quant(a)
-            for b, cp in late:
-                take_cols(b, cp)
+                quant(a)
+            for b, turned in late:
+                take_cols(col_sums[:, 4 * b : 4 * b + 4], turned[:])
             late = []
             for b, spread in spreads:
                 take_bias(b, spread)
@@ -379,38 +366,39 @@ def tile_two_layer_contrastive_similarity_s2_kernel(
             emit_loads(LOADS[s + 1] if s + 1 < len(LOADS) else 3)
             if s >= 2:
                 colsum(s - 2)
-            old = prev
+            old = [a for a in prev if TILES[a][0] == "x"]
             prev = TRANS_AFTER.get(s, [])
             for a in prev:
                 trans(a)
-            for a, at in PERM.items():
-                if at[0] == s:
-                    prep(a)
+            preps(s)
             for b, at in SPREAD.items():
                 if at == s:
                     spreads.append((b, spread_bias(b)))
             if s >= FINISH and s % 8 == FINISH % 8:
-                late.append((s // 8 - 1, finish_cols(s // 8 - 1, [sums[s // 8 - 1]])))
-            if s == 31:
-                colsum(30)
-                col_part = keep.tile([P, 4], F32, name="col_part")
-                cp = finish_cols(3, [sums[3], e_of[30]])
-        zadd(31, 0, 256)
-        exp(31, 0, 256)
-        store(31, 0, 256)
-        zadd(31, 256, 512)
-        exp(31, 256, 512)
-        store(31, 256, 512)
-        nc.vector.tensor_copy(out=col_part[:], in_=cp[:, 0:4])
+                turned = misc_pool.tile([P, 4, P], F32, name="misc")
+                turn_cols(sums[s // 8 - 1], turned)
+                late.append((s // 8 - 1, turned))
+        for h in range(2):
+            zadd(31, 256 * h, 256 * h + 256)
+            exp(31, 256 * h, 256 * h + 256)
+            store(31, 256 * h, 256 * h + 256)
+        turned_30 = acc_pool.tile([P, 4, P], F32, name="acc")
+        turn_cols(e_of[30], turned_30)
+        take_cols(parts[:, :, 0], turned_30[:])
+        turned_total = acc_pool.tile([P, 4, P], F32, name="acc")
+        turn_cols(sums[3], turned_total)
+        take_cols(parts[:, :, 1], turned_total[:])
+        for h in range(2):
+            turned_31 = tp_pool.tile([P, 4, P], F32, name="tp")
+            turn_cols(e_of[31], turned_31, 2 * h, 2 * h + 2)
+            take_cols(parts[:, 2 * h : 2 * h + 2, 2], turned_31[:, 2 * h : 2 * h + 2, :])
         nc.vector.tensor_reduce(out=row_total[:, 0:7], in_=row_sums[:], axis=X_AXIS, op=ADD)
-        colsum(31)
-        last = finish_cols(4, [e_of[31]])
-        nc.vector.tensor_tensor(out=col_sums[:, 12:16], in0=last[:, 0:4], in1=col_part[:], op=ADD)
+        take_cols(col_sums[:, 12:16], parts[:])
         nc.vector.tensor_reduce(out=row_total[:, 7:8], in_=last_sums[:], axis=X_AXIS, op=ADD)
         ct = acc_pool.tile([P, 512], F32, name="acc")
         nc.tensor.transpose(ct[:, 0:P], col_sums[:], ident[:])
         nc.vector.tensor_scalar(out=row_mean[:], in0=row_total[:], scalar1=1.0 / TEXTS, scalar2=None, op0=MULT)
         nc.sync.dma_start(out=out_1.rearrange("(p m) -> p m", m=IMG_TILES), in_=row_mean[:])
         col_mean = keep.tile([16, P], F32, name="col_mean")
-        nc.scalar.copy(out=col_mean[:], in_=ct[0:16, 0:P])
+        nc.scalar.activation(out=col_mean[:], in_=ct[0:16, 0:P], func=COPY, scale=1.0 / IMAGES)
         nc.sync.dma_start(out=out_2.rearrange("(c p) -> c p", p=P), in_=col_mean[:])

@@ -23,17 +23,18 @@ BLOCKS = TEXTS // 512
 FLOPS = 2 * IMAGES * TEXTS * (LAST + RES)
 
 TILES = [("x", 0), ("x", 1), ("i", 0), ("x", 2), ("x", 3)] + [("i", m) for m in range(1, 8)] + [("x", t) for t in range(4, 16)]
-HEAD = 6
-TRANS_AFTER = {0: [6], 1: [7, 8], 2: [9, 10], 4: [11, 14], 3: [12, 13], 5: [15], 7: [16], 12: [17, 18], 13: [19], 19: [20, 23], 20: [21], 15: [22]}
-PERM = {7: (0, 's'), 9: (1, 's'), 10: (1, 's'), 11: (3, 's'), 14: (3, 's'), 15: (4, 'v'), 16: (4, 's'), 17: (10, 'v'), 18: (10, 's'), 19: (11, 's'), 20: (16, 's'), 21: (19, 'v'), 23: (16, 's')}
-LOADS = [2, 2, 2, 3, 2]
-HEAD_BANKS = {0: "sv", 1: "sv", 3: "sv", 4: "sv"}
+HEAD = 5
+TRANS_AFTER = {0: [6], 1: [7], 2: [8], 3: [9, 12], 4: [10, 13], 5: [11, 14], 6: [15], 11: [16, 18], 12: [17], 13: [19], 16: [20], 18: [21], 19: [22], 21: [23]}
+PERM = {6: (-1, 'v'), 7: (0, 'v'), 8: (1, 'v'), 9: (2, 'v'), 10: (3, 'v'), 11: (4, 'v'), 13: (3, 'v'), 16: (10, 'v'), 17: (9, 's'), 18: (9, 'v'), 19: (10, 'v'), 20: (14, 's'), 22: (18, 's'), 23: (18, 'v')}
+LOADS = [4, 2, 5, 8, 6]
 X_BUFS = 8
-Z_BUFS = 12
-BANKS = {6: 'ss', 7: 'vv', 8: 'sv', 9: 'vs', 10: 'sv', 11: 'vv', 12: 'vs', 13: 'vv', 14: 'ss', 15: 'ss', 16: 'ss', 17: 'vs', 18: 'ss', 19: 'ss', 20: 'vv', 21: 'ss', 22: 'ss', 23: 'ss'}
-SPREAD = {1: 3, 2: 1, 3: 7}
-COLSUM = [8, 8, 8, 5]
-FINISH = 12
+Z_BUFS = 9
+E_BUFS = 11
+BANKS = {0: 'vs', 1: 'ss', 2: 'ss', 3: 'ss', 4: 'ss', 5: 'ss', 6: 'ss', 7: 'ss', 8: 'ss', 9: 'ss', 10: 'sv', 11: 'ss', 12: 'sv', 13: 'ss', 14: 'ss', 15: 'ss', 16: 'vs', 17: 'ss', 18: 'vv', 19: 'sv', 20: 'sv', 21: 'vv', 22: 'sv', 23: 'ss'}
+SPREAD = {1: 2, 2: 6, 3: 18}
+COLSUM = [8, 8, 8, 6]
+FINISH = [19, 21, 30]
+LAG = [2, 3, 0, 0]
 SINGLE = (0, 1, 2, 3)
 
 
@@ -44,10 +45,11 @@ def tile_two_layer_contrastive_similarity_s2_kernel(
     with ExitStack() as ctx:
         keep = ctx.enter_context(tc.tile_pool(name="keep", bufs=1))
         ring2 = ctx.enter_context(tc.tile_pool(name="ring2", bufs=2))
+        ring4 = ctx.enter_context(tc.tile_pool(name="ring4", bufs=3))
         ring3 = ctx.enter_context(tc.tile_pool(name="ring3", bufs=3))
         x_ring = ctx.enter_context(tc.tile_pool(name="x_ring", bufs=X_BUFS))
         z_ring = ctx.enter_context(tc.tile_pool(name="z_ring", bufs=Z_BUFS))
-        e_ring = ctx.enter_context(tc.tile_pool(name="e_ring", bufs=6))
+        e_ring = ctx.enter_context(tc.tile_pool(name="e_ring", bufs=E_BUFS))
         tp_pool = ctx.enter_context(tc.psum_pool(name="tp_pool", bufs=4))
         acc_pool = ctx.enter_context(tc.psum_pool(name="acc_pool", bufs=3))
         misc_pool = ctx.enter_context(tc.psum_pool(name="misc_pool", bufs=1))
@@ -83,20 +85,18 @@ def tile_two_layer_contrastive_similarity_s2_kernel(
 
         ident = keep.tile([P, P], F32, name="ident")
         make_identity(nc, ident[:])
-        warm = keep.tile([P, 1], F32, name="warm")
-        nc.vector.memset(warm[:], 0.0)
-        warm_out = keep.tile([P, 1], F32, name="warm_out")
-        nc.scalar.activation(out=warm_out[:], in_=warm[:], func=EXP)
-        factors = keep.tile([P, 12], BF16, name="factors", align_bytes=64)
-        nc.gpsimd.dma_start(
-            out=factors[:].rearrange("p (g t) -> p g t", t=4),
-            in_=gain.rearrange("(g p t) -> p g t", p=P, t=4),
-        )
-        bias_row = keep.tile([P, TEXTS], BF16, name="bias_row")
-        nc.vector.memset(bias_row[:], 0.0)
-        nc.gpsimd.dma_start(out=bias_row[0:1, :], in_=bias.rearrange("(o k) -> o k", o=1))
+        gain_row = keep.tile([P, RES], BF16, name="gain_row")
+        nc.vector.memset(gain_row[:], 0.0)
+        nc.scalar.dma_start(out=gain_row[0:1, :], in_=gain.rearrange("(o k) -> o k", o=1))
         ones = keep.tile([P, P], BF16, name="ones")
         nc.vector.memset(ones[:], 1.0)
+        warm = keep.tile([P, 1], F32, name="warm")
+        nc.vector.memset(warm[:], 0.0)
+        bias_row = keep.tile([P, TEXTS], BF16, name="bias_row")
+        nc.vector.memset(bias_row[:], 0.0)
+        nc.scalar.dma_start(out=bias_row[0:1, :], in_=bias.rearrange("(o k) -> o k", o=1))
+        warm_out = keep.tile([P, 1], F32, name="warm_out")
+        nc.scalar.activation(out=warm_out[:], in_=warm[:], func=EXP)
         col_sums = keep.tile([P, P], F32, name="col_sums")
         nc.vector.memset(col_sums[:], 0.0)
         load_xl(0, 0, 2)
@@ -118,6 +118,21 @@ def tile_two_layer_contrastive_similarity_s2_kernel(
 
         bias_b = keep.tile([P, TEXTS], BF16, name="bias_b", align_bytes=64)
 
+        gain_b = keep.tile([P, RES], BF16, name="gain_b", align_bytes=64)
+
+        def spread_gain(g):
+            acc = acc_pool.tile([P, 512], F32, name="acc")
+            nc.tensor.matmul(acc[:], ones[:], gain_row[:, g * 512 : (g + 1) * 512], start=True, stop=True)
+            return acc
+
+        def take_gain(g, acc):
+            nc.scalar.copy(
+                out=gain_b[:]
+                .rearrange("p (u k) -> p u k", u=2)[:, :, g * 256 : (g + 1) * 256]
+                .rearrange("p u (w e) -> p u w e", e=2),
+                in_=acc[:].rearrange("p (w u e) -> p u w e", u=2, e=2),
+            )
+
         def spread_bias(b):
             spread = misc_pool.tile([P, 512], F32, name="misc")
             nc.tensor.matmul(spread[:], ones[:], bias_row[:, b * 512 : (b + 1) * 512], start=True, stop=True)
@@ -136,20 +151,26 @@ def tile_two_layer_contrastive_similarity_s2_kernel(
 
         def prep(a):
             kind, n = TILES[a]
-            x_perm = ring3.tile([P, PASSES * 512], BF16, name="x_perm", align_bytes=64)
+            x_perm = ring4.tile([P, PASSES * 512], BF16, name="x_perm", align_bytes=64)
             ready[a] = x_perm
+            if kind == "i":
+                nc.vector.tensor_tensor(
+                    out=x_perm[:, 0:RES].rearrange("p (u w e) -> p u w e", u=2, e=2),
+                    in0=ir[n][:].rearrange("p (w u e) -> p u w e", u=2, e=2),
+                    in1=gain_b[:].rearrange("p (u w e) -> p u w e", u=2, e=2),
+                    op=MULT,
+                )
+                return
             copy = nc.scalar.copy if PERM[a][1] == "s" else nc.vector.tensor_copy
             words = x_perm[:].bitcast(F32)
-            if kind == "x":
-                b, i = divmod(n, 4)
-                copy(
-                    out=words[:, 768:1024].rearrange("p (u w) -> p u w", u=2),
-                    in_=xl[b][:, i * LAST : (i + 1) * LAST].bitcast(F32).rearrange("p (w u) -> p u w", u=2),
-                )
-            res = xr[n] if kind == "x" else ir[n]
+            b, i = divmod(n, 4)
+            copy(
+                out=words[:, 768:1024].rearrange("p (u w) -> p u w", u=2),
+                in_=xl[b][:, i * LAST : (i + 1) * LAST].bitcast(F32).rearrange("p (w u) -> p u w", u=2),
+            )
             copy(
                 out=words[:, 0:768].rearrange("p (u w) -> p u w", u=2),
-                in_=res[:].bitcast(F32).rearrange("p (w u) -> p u w", u=2),
+                in_=xr[n][:].bitcast(F32).rearrange("p (w u) -> p u w", u=2),
             )
 
         def words_of(a, g, u):
@@ -165,11 +186,15 @@ def tile_two_layer_contrastive_similarity_s2_kernel(
             if g == 0:
                 w = xl[b][:].bitcast(F32)
                 return w[:, i * 256 + u : (i + 1) * 256 : 2]
-            w = (xr[n] if kind == "x" else ir[n])[:].bitcast(F32)
+            w = xr[n][:].bitcast(F32)
             return w[:, (g - 1) * 256 + u : g * 256 : 2]
+
+        turned_texts = []
 
         def trans(a):
             banks[a] = []
+            if TILES[a][0] == "x":
+                turned_texts.append(TILES[a][1])
             for h in range(2):
                 tp = tp_pool.tile([P, 2, 2, P], F32, name="tp")
                 for u in range(2):
@@ -179,7 +204,7 @@ def tile_two_layer_contrastive_similarity_s2_kernel(
 
         def copies(a, only):
             kind, n = TILES[a]
-            engines = BANKS[a] if a in BANKS else HEAD_BANKS.get(a, "")
+            engines = BANKS[a]
             single = kind == "i" or n in SINGLE
             key, r0 = (a, 0) if single else (("pair", n // 2), (n % 2) * P)
             if key not in grouped_of:
@@ -188,21 +213,6 @@ def tile_two_layer_contrastive_similarity_s2_kernel(
                 else:
                     grouped_of[key] = ring2.tile([P, PASSES * 1024], BF16, name="grouped2", align_bytes=64)
             words = grouped_of[key][:].bitcast(F32).rearrange("p (g r u) -> p g r u", g=PASSES, u=2)
-            if kind == "i":
-                if only == "s":
-                    nc.scalar.copy(out=words[:, 0], in_=banks[a][0][:, :, 0, :].rearrange("p u r -> p r u"))
-                    return
-                out = grouped_of[key][:].rearrange("p (g r u e) -> p g r u e", g=PASSES, u=2, e=2)
-                for h, j in ((0, 1), (1, 0)):
-                    g0, g1 = 2 * h + j, 2 * h + 2
-                    f = factors[:, 4 * g0 - 4 : 4 * g1 - 4].rearrange("p (g o u e) -> p g o u e", o=1, u=2, e=2)
-                    nc.vector.tensor_tensor(
-                        out=out[:, g0:g1],
-                        in0=banks[a][h][:, :, j:2, :].bitcast(BF16).rearrange("p u g (r e) -> p g r u e", e=2),
-                        in1=f.to_broadcast([P, g1 - g0, P, 2, 2]),
-                        op=MULT,
-                    )
-                return
             for h in range(2):
                 if engines[h] == only:
                     copy = nc.scalar.copy if only == "s" else nc.vector.tensor_copy
@@ -288,12 +298,10 @@ def tile_two_layer_contrastive_similarity_s2_kernel(
             b, m = divmod(s, IMG_TILES)
             if m == 0 or s >= 30:
                 return
-            if m == 1:
-                first = e_of[s - 1]
-                total = ring2.tile([P, 512], F32, name="total")
-                sums[b] = total
-            else:
-                total = first = sums[b]
+            if b not in sums:
+                sums[b] = ring2.tile([P, 512], F32, name="total")
+            total = sums[b]
+            first = e_of[s - 1] if m == 1 else total
             eng = nc.gpsimd if m < COLSUM[b] else nc.vector
             eng.tensor_tensor(out=total[:, c0:c1], in0=first[:, c0:c1], in1=e_of[s][:, c0:c1], op=ADD)
 
@@ -304,15 +312,26 @@ def tile_two_layer_contrastive_similarity_s2_kernel(
         def take_cols(out, turned):
             nc.vector.tensor_reduce(out=out, in_=turned, axis=X_AXIS, op=ADD)
 
+        def preps(s):
+            for a in range(6, 24):
+                if a in PERM and PERM[a][0] == s:
+                    prep(a)
+
+        gains = [spread_gain(g) for g in range(3)]
+        for g in range(3):
+            take_gain(g, gains[g])
         for a in range(HEAD):
             trans(a)
-            if a == 4:
-                spread = spread_bias(0)
             copies(a, "s")
             copies(a, "v")
+            if a == 0:
+                prep(2)
+            if a == 3:
+                prep(5)
             quant(a)
-            if a == 4:
-                take_bias(0, spread)
+        trans(5)
+        spread = spread_bias(0)
+        preps(-1)
 
         pending = []
         for b in range(1, BLOCKS):
@@ -321,17 +340,17 @@ def tile_two_layer_contrastive_similarity_s2_kernel(
                 pending.append(("xr", 4 * b + i))
 
         def emit_loads(count):
-            for kind, n in pending[:count]:
+            for i in range(count):
+                if not pending:
+                    return
+                kind, n = pending[0]
                 if kind == "xl":
                     load_xl(n, 0, 4)
-                else:
+                elif n < X_BUFS or n - X_BUFS in turned_texts:
                     load_xr(n)
-            pending[:count] = []
-
-        def preps(s):
-            for a in range(6, 24):
-                if a in PERM and PERM[a][0] == s:
-                    prep(a)
+                else:
+                    return
+                pending.remove(pending[0])
 
         emit_loads(LOADS[0])
         prev = []
@@ -340,6 +359,11 @@ def tile_two_layer_contrastive_similarity_s2_kernel(
         spreads = []
         for s in range(32):
             mm(s)
+            if s == 0:
+                copies(5, "s")
+                copies(5, "v")
+                quant(5)
+                take_bias(0, spread)
             for a in prev:
                 copies(a, "s")
             for a in prev:
@@ -355,8 +379,6 @@ def tile_two_layer_contrastive_similarity_s2_kernel(
             for a in prev:
                 if TILES[a][0] == "x":
                     copies(a, "v")
-            for a in old:
-                quant(a)
             for b, turned in late:
                 take_cols(col_sums[:, 4 * b : 4 * b + 4], turned[:])
             late = []
@@ -364,20 +386,24 @@ def tile_two_layer_contrastive_similarity_s2_kernel(
                 take_bias(b, spread)
             spreads = []
             emit_loads(LOADS[s + 1] if s + 1 < len(LOADS) else 3)
-            if s >= 2:
-                colsum(s - 2)
+            for n in range(30):
+                if n + 2 + LAG[n // 8] == s:
+                    colsum(n)
             old = [a for a in prev if TILES[a][0] == "x"]
             prev = TRANS_AFTER.get(s, [])
             for a in prev:
                 trans(a)
             preps(s)
+            for a in old:
+                quant(a)
             for b, at in SPREAD.items():
                 if at == s:
                     spreads.append((b, spread_bias(b)))
-            if s >= FINISH and s % 8 == FINISH % 8:
-                turned = misc_pool.tile([P, 4, P], F32, name="misc")
-                turn_cols(sums[s // 8 - 1], turned)
-                late.append((s // 8 - 1, turned))
+            for b in range(3):
+                if FINISH[b] == s:
+                    turned = misc_pool.tile([P, 4, P], F32, name="misc")
+                    turn_cols(sums[b], turned)
+                    late.append((b, turned))
         for h in range(2):
             zadd(31, 256 * h, 256 * h + 256)
             exp(31, 256 * h, 256 * h + 256)

@@ -24,17 +24,17 @@ FLOPS = 2 * IMAGES * TEXTS * (LAST + RES)
 
 TILES = [("x", 0), ("x", 1), ("i", 0), ("x", 2), ("x", 3)] + [("i", m) for m in range(1, 8)] + [("x", t) for t in range(4, 16)]
 HEAD = 5
-TRANS_AFTER = {0: [6], 1: [7], 2: [8], 3: [9, 12], 4: [10, 13], 5: [11, 14], 6: [15], 11: [16, 18], 12: [17], 13: [19], 16: [20], 18: [21], 19: [22], 21: [23]}
-PERM = {6: (-1, 'v'), 7: (0, 'v'), 8: (1, 'v'), 9: (2, 'v'), 10: (3, 'v'), 11: (4, 'v'), 13: (3, 'v'), 16: (10, 'v'), 17: (9, 's'), 18: (9, 'v'), 19: (10, 'v'), 20: (14, 's'), 22: (18, 's'), 23: (18, 'v')}
-LOADS = [4, 2, 5, 8, 6]
+TRANS_AFTER = {0: [6], 1: [7], 2: [8, 9], 4: [10], 5: [11, 14], 3: [12], 6: [13, 15], 8: [16], 13: [17, 19], 7: [18], 14: [20], 21: [21, 23], 15: [22]}
+PERM = {6: (-1, 'v'), 7: (0, 'v'), 8: (1, 'v'), 9: (1, 'v'), 10: (3, 'v'), 11: (4, 'v'), 12: (2, 'v'), 13: (5, 'v'), 14: (4, 's'), 16: (7, 's'), 17: (11, 'v'), 19: (10, 's'), 20: (11, 's'), 21: (19, 's'), 22: (13, 's')}
+LOADS = [4, 8, 8, 4, 8]
 X_BUFS = 8
 Z_BUFS = 9
 E_BUFS = 11
-BANKS = {0: 'vs', 1: 'ss', 2: 'ss', 3: 'ss', 4: 'ss', 5: 'ss', 6: 'ss', 7: 'ss', 8: 'ss', 9: 'ss', 10: 'sv', 11: 'ss', 12: 'sv', 13: 'ss', 14: 'ss', 15: 'ss', 16: 'vs', 17: 'ss', 18: 'vv', 19: 'sv', 20: 'sv', 21: 'vv', 22: 'sv', 23: 'ss'}
-SPREAD = {1: 2, 2: 6, 3: 18}
-COLSUM = [8, 8, 8, 6]
-FINISH = [19, 21, 30]
-LAG = [2, 3, 0, 0]
+BANKS = {0: 'sv', 1: 'ss', 2: 'ss', 3: 'ss', 4: 'ss', 5: 'ss', 6: 'ss', 7: 'ss', 8: 'vs', 9: 'ss', 10: 'vs', 11: 'ss', 12: 'vs', 13: 'vv', 14: 'ss', 15: 'ss', 16: 'sv', 17: 'vv', 18: 'vs', 19: 'sv', 20: 'vs', 21: 'sv', 22: 'ss', 23: 'ss'}
+SPREAD = {1: 6, 2: 2, 3: 1}
+COLSUM = [7, 7, 7, 2]
+FINISH = [15, 25, 30]
+LAG = [1, 2, 1, 0]
 SINGLE = (0, 1, 2, 3)
 
 
@@ -87,20 +87,20 @@ def tile_two_layer_contrastive_similarity_s2_kernel(
         make_identity(nc, ident[:])
         gain_row = keep.tile([P, RES], BF16, name="gain_row")
         nc.vector.memset(gain_row[:], 0.0)
-        nc.scalar.dma_start(out=gain_row[0:1, :], in_=gain.rearrange("(o k) -> o k", o=1))
         ones = keep.tile([P, P], BF16, name="ones")
         nc.vector.memset(ones[:], 1.0)
         warm = keep.tile([P, 1], F32, name="warm")
         nc.vector.memset(warm[:], 0.0)
         bias_row = keep.tile([P, TEXTS], BF16, name="bias_row")
         nc.vector.memset(bias_row[:], 0.0)
-        nc.scalar.dma_start(out=bias_row[0:1, :], in_=bias.rearrange("(o k) -> o k", o=1))
+        nc.gpsimd.dma_start(out=bias_row[0:1, :], in_=bias.rearrange("(o k) -> o k", o=1))
         warm_out = keep.tile([P, 1], F32, name="warm_out")
         nc.scalar.activation(out=warm_out[:], in_=warm[:], func=EXP)
         col_sums = keep.tile([P, P], F32, name="col_sums")
         nc.vector.memset(col_sums[:], 0.0)
         load_xl(0, 0, 2)
         load_xr(0)
+        nc.sync.dma_start(out=gain_row[0:1, :], in_=gain.rearrange("(o k) -> o k", o=1))
         load_xr(1)
         load_il(0, 2)
         load_ir(0)
@@ -126,12 +126,8 @@ def tile_two_layer_contrastive_similarity_s2_kernel(
             return acc
 
         def take_gain(g, acc):
-            nc.scalar.copy(
-                out=gain_b[:]
-                .rearrange("p (u k) -> p u k", u=2)[:, :, g * 256 : (g + 1) * 256]
-                .rearrange("p u (w e) -> p u w e", e=2),
-                in_=acc[:].rearrange("p (w u e) -> p u w e", u=2, e=2),
-            )
+            copy = nc.vector.tensor_copy if g == 1 else nc.scalar.copy
+            copy(out=gain_b[:, g * 512 : (g + 1) * 512], in_=acc[:])
 
         def spread_bias(b):
             spread = misc_pool.tile([P, 512], F32, name="misc")
@@ -154,12 +150,7 @@ def tile_two_layer_contrastive_similarity_s2_kernel(
             x_perm = ring4.tile([P, PASSES * 512], BF16, name="x_perm", align_bytes=64)
             ready[a] = x_perm
             if kind == "i":
-                nc.vector.tensor_tensor(
-                    out=x_perm[:, 0:RES].rearrange("p (u w e) -> p u w e", u=2, e=2),
-                    in0=ir[n][:].rearrange("p (w u e) -> p u w e", u=2, e=2),
-                    in1=gain_b[:].rearrange("p (u w e) -> p u w e", u=2, e=2),
-                    op=MULT,
-                )
+                nc.vector.tensor_tensor(out=x_perm[:, 0:RES], in0=ir[n][:], in1=gain_b[:], op=MULT)
                 return
             copy = nc.scalar.copy if PERM[a][1] == "s" else nc.vector.tensor_copy
             words = x_perm[:].bitcast(F32)
@@ -178,6 +169,9 @@ def tile_two_layer_contrastive_similarity_s2_kernel(
             if kind == "i" and g == 0:
                 w = il[:].bitcast(F32)
                 return w[:, n * 256 + u : (n + 1) * 256 : 2]
+            if kind == "i":
+                w = ready[a][:].bitcast(F32)
+                return w[:, (g - 1) * 256 + u : g * 256 : 2]
             if a in ready:
                 w = ready[a][:].bitcast(F32)
                 k = 768 + u * P if g == 0 else u * 384 + (g - 1) * P
@@ -317,14 +311,14 @@ def tile_two_layer_contrastive_similarity_s2_kernel(
                 if a in PERM and PERM[a][0] == s:
                     prep(a)
 
-        gains = [spread_gain(g) for g in range(3)]
-        for g in range(3):
-            take_gain(g, gains[g])
         for a in range(HEAD):
             trans(a)
             copies(a, "s")
             copies(a, "v")
             if a == 0:
+                gains = [spread_gain(g) for g in range(3)]
+                for g in range(3):
+                    take_gain(g, gains[g])
                 prep(2)
             if a == 3:
                 prep(5)

from contextlib import ExitStack

import concourse.mybir as mybir
from concourse.masks import make_identity

F32 = mybir.dt.float32
BF16 = mybir.dt.bfloat16
U32 = mybir.dt.uint32
U8 = mybir.dt.uint8
E4M3 = mybir.dt.float8_e4m3fn_x4
E5M2 = mybir.dt.float8_e5m2_x4
ADD = mybir.AluOpType.add
MULT = mybir.AluOpType.mult
COPY = mybir.ActivationFunctionType.Copy
EXP = mybir.ActivationFunctionType.Exp
X_AXIS = mybir.AxisListType.X

P = 128
IMAGES, TEXTS, LAST, RES = 1024, 2048, 512, 1536
PASSES = (LAST + RES) // 512
IMG_TILES = IMAGES // P
BLOCKS = TEXTS // 512
FLOPS = 2 * IMAGES * TEXTS * (LAST + RES)

TILES = [("x", 0), ("x", 1), ("i", 0), ("x", 2), ("x", 3)] + [("i", m) for m in range(1, 8)] + [("x", t) for t in range(4, 16)]
HEAD = 5
TRANS_AFTER = {0: [6], 1: [7], 2: [8, 9], 4: [10], 5: [11, 14], 3: [12], 6: [13, 15], 8: [16], 13: [17, 19], 7: [18], 14: [20], 21: [21, 23], 15: [22]}
PERM = {6: (-1, 'v'), 7: (0, 'v'), 8: (1, 'v'), 9: (1, 'v'), 10: (3, 'v'), 11: (4, 'v'), 12: (2, 'v'), 13: (5, 'v'), 14: (4, 's'), 16: (7, 's'), 17: (11, 'v'), 19: (10, 's'), 20: (11, 's'), 21: (19, 's'), 22: (13, 's')}
LOADS = [4, 8, 8, 4, 8]
X_BUFS = 8
Z_BUFS = 9
E_BUFS = 11
BANKS = {0: 'sv', 1: 'ss', 2: 'ss', 3: 'ss', 4: 'ss', 5: 'ss', 6: 'ss', 7: 'ss', 8: 'vs', 9: 'ss', 10: 'vs', 11: 'ss', 12: 'vs', 13: 'vv', 14: 'ss', 15: 'ss', 16: 'sv', 17: 'vv', 18: 'vs', 19: 'sv', 20: 'vs', 21: 'sv', 22: 'ss', 23: 'ss'}
SPREAD = {1: 6, 2: 2, 3: 1}
COLSUM = [7, 7, 7, 2]
FINISH = [15, 25, 30]
LAG = [1, 2, 1, 0]
SINGLE = (0, 1, 2, 3)


def tile_two_layer_contrastive_similarity_s2_kernel(
    tc, img_last, img_res, gain, txt_last, txt_res, bias, out_0, out_1, out_2
):
    nc = tc.nc
    with ExitStack() as ctx:
        keep = ctx.enter_context(tc.tile_pool(name="keep", bufs=1))
        ring2 = ctx.enter_context(tc.tile_pool(name="ring2", bufs=2))
        ring4 = ctx.enter_context(tc.tile_pool(name="ring4", bufs=3))
        ring3 = ctx.enter_context(tc.tile_pool(name="ring3", bufs=3))
        x_ring = ctx.enter_context(tc.tile_pool(name="x_ring", bufs=X_BUFS))
        z_ring = ctx.enter_context(tc.tile_pool(name="z_ring", bufs=Z_BUFS))
        e_ring = ctx.enter_context(tc.tile_pool(name="e_ring", bufs=E_BUFS))
        tp_pool = ctx.enter_context(tc.psum_pool(name="tp_pool", bufs=4))
        acc_pool = ctx.enter_context(tc.psum_pool(name="acc_pool", bufs=3))
        misc_pool = ctx.enter_context(tc.psum_pool(name="misc_pool", bufs=1))
        ctx.enter_context(tc.manual_schedule())

        xl = [keep.tile([P, 4 * LAST], BF16, name=f"xl{b}", align_bytes=64) for b in range(BLOCKS)]
        xr = {}
        il = keep.tile([P, IMG_TILES * LAST], BF16, name="il", align_bytes=64)
        ir = [keep.tile([P, RES], BF16, name=f"ir{m}", align_bytes=64) for m in range(IMG_TILES)]
        img_last_v = img_last.rearrange("(p m) k -> p m k", m=IMG_TILES)
        img_res_v = img_res.rearrange("(p m) k -> p m k", m=IMG_TILES)
        out_v = out_0.rearrange("(p m) j -> p m j", m=IMG_TILES)

        def load_xl(b, i0, i1):
            nc.sync.dma_start(
                out=xl[b][:, i0 * LAST : i1 * LAST].rearrange("p (i k) -> p i k", k=LAST),
                in_=txt_last[b * 512 + i0 * P : b * 512 + i1 * P, :].rearrange("(i p) k -> p i k", p=P),
            )

        def load_xr(t):
            x_res = x_ring.tile([P, RES], BF16, name="x_res", align_bytes=64)
            xr[t] = x_res
            nc.sync.dma_start(out=xr[t][:], in_=txt_res[t * P : (t + 1) * P, :])

        def load_il(m0, m1):
            nc.sync.dma_start(
                out=il[:, m0 * LAST : m1 * LAST].rearrange("p (m k) -> p m k", k=LAST),
                in_=img_last_v[:, m0:m1, :],
            )

        def load_ir(m):
            nc.sync.dma_start(out=ir[m][:], in_=img_res_v[:, m, :])

        ident = keep.tile([P, P], F32, name="ident")
        make_identity(nc, ident[:])
        gain_row = keep.tile([P, RES], BF16, name="gain_row")
        nc.vector.memset(gain_row[:], 0.0)
        ones = keep.tile([P, P], BF16, name="ones")
        nc.vector.memset(ones[:], 1.0)
        warm = keep.tile([P, 1], F32, name="warm")
        nc.vector.memset(warm[:], 0.0)
        bias_row = keep.tile([P, TEXTS], BF16, name="bias_row")
        nc.vector.memset(bias_row[:], 0.0)
        nc.gpsimd.dma_start(out=bias_row[0:1, :], in_=bias.rearrange("(o k) -> o k", o=1))
        warm_out = keep.tile([P, 1], F32, name="warm_out")
        nc.scalar.activation(out=warm_out[:], in_=warm[:], func=EXP)
        col_sums = keep.tile([P, P], F32, name="col_sums")
        nc.vector.memset(col_sums[:], 0.0)
        load_xl(0, 0, 2)
        load_xr(0)
        nc.sync.dma_start(out=gain_row[0:1, :], in_=gain.rearrange("(o k) -> o k", o=1))
        load_xr(1)
        load_il(0, 2)
        load_ir(0)
        load_xl(0, 2, 4)
        load_xr(2)
        load_xr(3)

        load_ir(1)
        load_il(2, 4)
        load_ir(2)
        load_ir(3)
        load_il(4, 8)
        for m in range(4, 8):
            load_ir(m)

        bias_b = keep.tile([P, TEXTS], BF16, name="bias_b", align_bytes=64)

        gain_b = keep.tile([P, RES], BF16, name="gain_b", align_bytes=64)

        def spread_gain(g):
            acc = acc_pool.tile([P, 512], F32, name="acc")
            nc.tensor.matmul(acc[:], ones[:], gain_row[:, g * 512 : (g + 1) * 512], start=True, stop=True)
            return acc

        def take_gain(g, acc):
            copy = nc.vector.tensor_copy if g == 1 else nc.scalar.copy
            copy(out=gain_b[:, g * 512 : (g + 1) * 512], in_=acc[:])

        def spread_bias(b):
            spread = misc_pool.tile([P, 512], F32, name="misc")
            nc.tensor.matmul(spread[:], ones[:], bias_row[:, b * 512 : (b + 1) * 512], start=True, stop=True)
            return spread

        def take_bias(b, spread):
            nc.scalar.copy(out=bias_b[:, b * 512 : (b + 1) * 512], in_=spread[:])

        x_codes = [keep.tile([P, PASSES, 512], U32, name=f"xc{b}", align_bytes=64) for b in range(BLOCKS)]
        x_scales = [keep.tile([P, PASSES, 512], U8, name=f"xs{b}", align_bytes=64) for b in range(BLOCKS)]
        i_codes = [keep.tile([P, PASSES, P], U32, name=f"ic{m}", align_bytes=64) for m in range(IMG_TILES)]
        i_scales = [keep.tile([P, PASSES, P], U8, name=f"is{m}", align_bytes=64) for m in range(IMG_TILES)]
        ready = {}
        banks = {}
        grouped_of = {}

        def prep(a):
            kind, n = TILES[a]
            x_perm = ring4.tile([P, PASSES * 512], BF16, name="x_perm", align_bytes=64)
            ready[a] = x_perm
            if kind == "i":
                nc.vector.tensor_tensor(out=x_perm[:, 0:RES], in0=ir[n][:], in1=gain_b[:], op=MULT)
                return
            copy = nc.scalar.copy if PERM[a][1] == "s" else nc.vector.tensor_copy
            words = x_perm[:].bitcast(F32)
            b, i = divmod(n, 4)
            copy(
                out=words[:, 768:1024].rearrange("p (u w) -> p u w", u=2),
                in_=xl[b][:, i * LAST : (i + 1) * LAST].bitcast(F32).rearrange("p (w u) -> p u w", u=2),
            )
            copy(
                out=words[:, 0:768].rearrange("p (u w) -> p u w", u=2),
                in_=xr[n][:].bitcast(F32).rearrange("p (w u) -> p u w", u=2),
            )

        def words_of(a, g, u):
            kind, n = TILES[a]
            if kind == "i" and g == 0:
                w = il[:].bitcast(F32)
                return w[:, n * 256 + u : (n + 1) * 256 : 2]
            if kind == "i":
                w = ready[a][:].bitcast(F32)
                return w[:, (g - 1) * 256 + u : g * 256 : 2]
            if a in ready:
                w = ready[a][:].bitcast(F32)
                k = 768 + u * P if g == 0 else u * 384 + (g - 1) * P
                return w[:, k : k + P]
            b, i = divmod(n, 4)
            if g == 0:
                w = xl[b][:].bitcast(F32)
                return w[:, i * 256 + u : (i + 1) * 256 : 2]
            w = xr[n][:].bitcast(F32)
            return w[:, (g - 1) * 256 + u : g * 256 : 2]

        turned_texts = []

        def trans(a):
            banks[a] = []
            if TILES[a][0] == "x":
                turned_texts.append(TILES[a][1])
            for h in range(2):
                tp = tp_pool.tile([P, 2, 2, P], F32, name="tp")
                for u in range(2):
                    for j in range(2):
                        nc.tensor.transpose(tp[:, u, j, :], words_of(a, 2 * h + j, u), ident[:])
                banks[a].append(tp)

        def copies(a, only):
            kind, n = TILES[a]
            engines = BANKS[a]
            single = kind == "i" or n in SINGLE
            key, r0 = (a, 0) if single else (("pair", n // 2), (n % 2) * P)
            if key not in grouped_of:
                if single:
                    grouped_of[key] = ring3.tile([P, PASSES * 512], BF16, name="grouped1", align_bytes=64)
                else:
                    grouped_of[key] = ring2.tile([P, PASSES * 1024], BF16, name="grouped2", align_bytes=64)
            words = grouped_of[key][:].bitcast(F32).rearrange("p (g r u) -> p g r u", g=PASSES, u=2)
            for h in range(2):
                if engines[h] == only:
                    copy = nc.scalar.copy if only == "s" else nc.vector.tensor_copy
                    copy(
                        out=words[:, 2 * h : 2 * h + 2, r0 : r0 + P, :],
                        in_=banks[a][h][:].rearrange("p u g r -> p g r u"),
                    )

        def quant(a):
            kind, n = TILES[a]
            if kind == "x":
                if n % 2 == 0 and n not in SINGLE:
                    return
                b, i = divmod(n, 4)
                if n in SINGLE:
                    grouped, c0 = grouped_of[a], i * P
                else:
                    grouped, c0 = grouped_of["pair", n // 2], (i - 1) * P
                c1 = (i + 1) * P
                width = (c1 - c0) * 4
                for g in range(PASSES):
                    nc.vector.quantize_mx(
                        out=x_codes[b][:, g, c0:c1].bitcast(E4M3),
                        scales=x_scales[b][:, g, c0:c1],
                        in_=grouped[:, g * width : (g + 1) * width],
                    )
            else:
                grouped = grouped_of[a]
                codes = i_codes[n][:].rearrange("p g r -> p (g r)")
                scales = i_scales[n][:].rearrange("p g r -> p (g r)")
                for g0, g1, fmt in ((0, 1, E4M3), (1, 3, E5M2), (3, 4, E5M2)):
                    nc.vector.quantize_mx(
                        out=codes[:, g0 * P : g1 * P].bitcast(fmt),
                        scales=scales[:, g0 * P : g1 * P],
                        in_=grouped[:, g0 * 512 : g1 * 512],
                    )

        acc_of = {}
        z_of = {}
        e_of = {}
        sums = {}
        row_sums = keep.tile([P, 7, BLOCKS], F32, name="row_sums")
        last_sums = keep.tile([P, 5], F32, name="last_sums")
        parts = keep.tile([P, 4, 3], F32, name="parts")
        row_total = keep.tile([P, IMG_TILES], F32, name="row_total")
        row_mean = keep.tile([P, IMG_TILES], F32, name="row_mean")

        def mm(s):
            b, m = divmod(s, IMG_TILES)
            acc = acc_pool.tile([P, 512], F32, name="acc")
            for g in range(PASSES):
                nc.tensor.matmul_mx(
                    out=acc[:],
                    lhsT=i_codes[m][:, g, :].bitcast(E4M3 if g == 0 else E5M2),
                    lhsT_scale=i_scales[m][:, g, :],
                    rhs=x_codes[b][:, g, :].bitcast(E4M3),
                    rhs_scale=x_scales[b][:, g, :],
                    start=(g == 0),
                    stop=(g == PASSES - 1),
                )
            acc_of[s] = acc

        def zadd(s, c0=0, c1=512):
            b, m = divmod(s, IMG_TILES)
            if s not in z_of:
                z_of[s] = z_ring.tile([P, 512], F32, name="z")
            nc.vector.tensor_tensor(
                out=z_of[s][:, c0:c1], in0=acc_of[s][:, c0:c1], in1=bias_b[:, b * 512 + c0 : b * 512 + c1], op=ADD
            )

        def exp(s, c0=0, c1=512):
            b, m = divmod(s, IMG_TILES)
            if s not in e_of:
                e_of[s] = e_ring.tile([P, 512], F32, name="e")
            part = last_sums[:, b + c0 // 256 : b + c0 // 256 + 1] if m == 7 else row_sums[:, m, b : b + 1]
            nc.scalar.activation(out=e_of[s][:, c0:c1], in_=z_of[s][:, c0:c1], func=EXP, accum_out=part)

        def store(s, c0=0, c1=512):
            b, m = divmod(s, IMG_TILES)
            nc.sync.dma_start(out=out_v[:, m, b * 512 + c0 : b * 512 + c1], in_=z_of[s][:, c0:c1])

        def colsum(s, c0=0, c1=512):
            b, m = divmod(s, IMG_TILES)
            if m == 0 or s >= 30:
                return
            if b not in sums:
                sums[b] = ring2.tile([P, 512], F32, name="total")
            total = sums[b]
            first = e_of[s - 1] if m == 1 else total
            eng = nc.gpsimd if m < COLSUM[b] else nc.vector
            eng.tensor_tensor(out=total[:, c0:c1], in0=first[:, c0:c1], in1=e_of[s][:, c0:c1], op=ADD)

        def turn_cols(source, turned, c0=0, c1=4):
            for c in range(c0, c1):
                nc.tensor.transpose(turned[:, c, :], source[:, c * P : (c + 1) * P], ident[:])

        def take_cols(out, turned):
            nc.vector.tensor_reduce(out=out, in_=turned, axis=X_AXIS, op=ADD)

        def preps(s):
            for a in range(6, 24):
                if a in PERM and PERM[a][0] == s:
                    prep(a)

        for a in range(HEAD):
            trans(a)
            copies(a, "s")
            copies(a, "v")
            if a == 0:
                gains = [spread_gain(g) for g in range(3)]
                for g in range(3):
                    take_gain(g, gains[g])
                prep(2)
            if a == 3:
                prep(5)
            quant(a)
        trans(5)
        spread = spread_bias(0)
        preps(-1)

        pending = []
        for b in range(1, BLOCKS):
            pending.append(("xl", b))
            for i in range(4):
                pending.append(("xr", 4 * b + i))

        def emit_loads(count):
            for i in range(count):
                if not pending:
                    return
                kind, n = pending[0]
                if kind == "xl":
                    load_xl(n, 0, 4)
                elif n < X_BUFS or n - X_BUFS in turned_texts:
                    load_xr(n)
                else:
                    return
                pending.remove(pending[0])

        emit_loads(LOADS[0])
        prev = []
        old = []
        late = []
        spreads = []
        for s in range(32):
            mm(s)
            if s == 0:
                copies(5, "s")
                copies(5, "v")
                quant(5)
                take_bias(0, spread)
            for a in prev:
                copies(a, "s")
            for a in prev:
                if TILES[a][0] == "i":
                    copies(a, "v")
            if s >= 1:
                zadd(s - 1)
                exp(s - 1)
                store(s - 1)
            for a in prev:
                if TILES[a][0] == "i":
                    quant(a)
            for a in prev:
                if TILES[a][0] == "x":
                    copies(a, "v")
            for b, turned in late:
                take_cols(col_sums[:, 4 * b : 4 * b + 4], turned[:])
            late = []
            for b, spread in spreads:
                take_bias(b, spread)
            spreads = []
            emit_loads(LOADS[s + 1] if s + 1 < len(LOADS) else 3)
            for n in range(30):
                if n + 2 + LAG[n // 8] == s:
                    colsum(n)
            old = [a for a in prev if TILES[a][0] == "x"]
            prev = TRANS_AFTER.get(s, [])
            for a in prev:
                trans(a)
            preps(s)
            for a in old:
                quant(a)
            for b, at in SPREAD.items():
                if at == s:
                    spreads.append((b, spread_bias(b)))
            for b in range(3):
                if FINISH[b] == s:
                    turned = misc_pool.tile([P, 4, P], F32, name="misc")
                    turn_cols(sums[b], turned)
                    late.append((b, turned))
        for h in range(2):
            zadd(31, 256 * h, 256 * h + 256)
            exp(31, 256 * h, 256 * h + 256)
            store(31, 256 * h, 256 * h + 256)
        turned_30 = acc_pool.tile([P, 4, P], F32, name="acc")
        turn_cols(e_of[30], turned_30)
        take_cols(parts[:, :, 0], turned_30[:])
        turned_total = acc_pool.tile([P, 4, P], F32, name="acc")
        turn_cols(sums[3], turned_total)
        take_cols(parts[:, :, 1], turned_total[:])
        for h in range(2):
            turned_31 = tp_pool.tile([P, 4, P], F32, name="tp")
            turn_cols(e_of[31], turned_31, 2 * h, 2 * h + 2)
            take_cols(parts[:, 2 * h : 2 * h + 2, 2], turned_31[:, 2 * h : 2 * h + 2, :])
        nc.vector.tensor_reduce(out=row_total[:, 0:7], in_=row_sums[:], axis=X_AXIS, op=ADD)
        take_cols(col_sums[:, 12:16], parts[:])
        nc.vector.tensor_reduce(out=row_total[:, 7:8], in_=last_sums[:], axis=X_AXIS, op=ADD)
        ct = acc_pool.tile([P, 512], F32, name="acc")
        nc.tensor.transpose(ct[:, 0:P], col_sums[:], ident[:])
        nc.vector.tensor_scalar(out=row_mean[:], in0=row_total[:], scalar1=1.0 / TEXTS, scalar2=None, op0=MULT)
        nc.sync.dma_start(out=out_1.rearrange("(p m) -> p m", m=IMG_TILES), in_=row_mean[:])
        col_mean = keep.tile([16, P], F32, name="col_mean")
        nc.scalar.activation(out=col_mean[:], in_=ct[0:16, 0:P], func=COPY, scale=1.0 / IMAGES)
        nc.sync.dma_start(out=out_2.rearrange("(c p) -> c p", p=P), in_=col_mean[:])
